import numpy as np
import ml_dtypes


def mxq(x, axis, fmt="e4m3"):
    dtype, down = {"e4m3": (ml_dtypes.float8_e4m3fn, 7), "e5m2": (ml_dtypes.float8_e5m2, 14)}[fmt]
    v = np.moveaxis(np.asarray(x, np.float32).astype(ml_dtypes.bfloat16).astype(np.float64), axis, -1)
    blocks = v.reshape(v.shape[:-1] + (-1, 32))
    amax = np.abs(blocks).max(-1, keepdims=True)
    byte = np.maximum(np.where(amax > 0, np.frexp(amax)[1] - 1 + 127, 0) - down, 1)
    scale = np.exp2(byte - 127.0)
    codes = (blocks / scale).astype(np.float32).astype(dtype).astype(np.float64)
    return np.moveaxis((codes * scale).reshape(v.shape), -1, axis)


WIDE = False


def mx_kscale(k):
    if not WIDE:
        return np.ones(k)
    levels = np.array([10, -10, 5, -5, 0])
    if k % 512:
        return np.exp2(np.random.permutation(np.resize(levels, k // 32))).repeat(32)
    a = np.empty((k // 512, 16))
    for p in range(k // 512):
        a[p, :8] = np.random.permutation(np.resize(levels, 8))
        for g in range(8):
            far = levels[np.abs(levels - a[p, g]) >= 10]
            a[p, g + 8] = far[np.random.randint(len(far))]
    return np.exp2(a.ravel()).repeat(32)


def f64(x):
    return np.asarray(x).astype(np.float64)


def striped(idx):
    return np.tile(np.asarray(idx).reshape(-1, 16).T, (8, 1)).astype(np.uint16)


def unstriped(offs):
    return offs[:16].T.reshape(-1).astype(np.int64)


B, N, C, D, NQ = 1, 1024, 2048, 1024, 128


def eight(codes):
    return np.concatenate([codes[h].reshape(-1, 16).T for h in range(8)]).astype(np.uint16)


def uneight(offs):
    return np.stack([offs[16 * h:16 * h + 16].T.reshape(-1) for h in range(8)]).astype(np.int64)


def setup_inputs():
    n = np.random.standard_normal
    s = mx_kscale(D)[:, None]
    grid = lambda x: np.round(x * 32) / 32
    return {
        "qT": (n((B, D, NQ)) * s / np.sqrt(D)).astype(np.float32),
        "cb": (grid(n((D, C))) / s).astype(np.float32),
        "norm": np.tile(np.random.randint(32, 129, N) / 64.0, (128, 1)).astype(np.float32),
        "offs": eight(np.random.randint(0, C, (8, N))),
        "offs2": eight(np.random.randint(0, C, (8, N))),
    }


def reference(qT, cb, norm, offs, offs2):
    k = []
    for part, offs_ in enumerate((offs, offs2,)):
        codes = uneight(offs_)
        k += [f64(cb)[512 * part + 64 * h:512 * part + 64 * h + 64][:, codes[h]] for h in range(8)]
    k = np.concatenate(k) * f64(norm)[:1]
    a = mxq(f64(qT), 1, "e4m3").transpose(0, 2, 1) @ mxq(k, 0, "e4m3")
    return a

@@ -1,0 +1,149 @@
+from contextlib import ExitStack
+
+import concourse.mybir as mybir
+from concourse.masks import make_identity
+
+F32 = mybir.dt.float32
+BF16 = mybir.dt.bfloat16
+U32 = mybir.dt.uint32
+U16 = mybir.dt.uint16
+U8 = mybir.dt.uint8
+FP8X4 = mybir.dt.float8_e4m3fn_x4
+MULT = mybir.AluOpType.mult
+
+P = 128
+PACK = 4
+D = 1024
+N = 1024
+NQ = 128
+CODES = 2048
+PASSES = D // (P * PACK)
+FLOPS = 2 * NQ * D * N
+
+PIECES = ((0, 512), (512, 256), (768, 128), (896, 128))
+
+
+def tile_attend_pq_att_kernel(tc, qT, cb, norm, offs, offs2, out):
+    nc = tc.nc
+    with ExitStack() as ctx:
+        hold = ctx.enter_context(tc.tile_pool(name="hold", bufs=1))
+        psum = ctx.enter_context(tc.psum_pool(name="psum", bufs=1))
+
+        lists = [hold.tile([P, N // 16], U16, name=f"list{g}") for g in range(PASSES)]
+        books = [[hold.tile([P, CODES], F32, name=f"book{g}_{t}") for t in range(PACK)] for g in range(PASSES)]
+        norm_row = hold.tile([P, 2, 4], F32, name="norm_row")
+        q_raw = hold.tile([P, PASSES, PACK, NQ], F32, name="q_raw")
+        ident = hold.tile([P, P], F32, name="ident")
+        norm_all = hold.tile([P, N], F32, name="norm_all")
+        raw = [hold.tile([P, PACK, N], F32, name=f"raw{g}") for g in range(PASSES)]
+        grouped = [hold.tile([P, N, PACK], BF16, name=f"grouped{g}", align_bytes=64) for g in range(PASSES)]
+        codes = [hold.tile([P, N], U32, name=f"codes{g}", align_bytes=64) for g in range(PASSES)]
+        scales = [hold.tile([P, N], U8, name=f"scales{g}", align_bytes=64) for g in range(PASSES)]
+        q_grouped = hold.tile([P, PASSES, NQ, PACK], BF16, name="q_grouped", align_bytes=64)
+        q_codes = hold.tile([P, PASSES, NQ], U32, name="q_codes", align_bytes=64)
+        q_scales = hold.tile([P, PASSES, NQ], U8, name="q_scales", align_bytes=64)
+        result = [hold.tile([P, width], F32, name=f"result{i}") for i, (n0, width) in enumerate(PIECES)]
+        norm_bank = [psum.tile([P, 4, P], F32, name=f"norm_bank{b}") for b in range(2)]
+        acc = [psum.tile([P, width], F32, name=f"acc{i}") for i, (n0, width) in enumerate(PIECES)]
+
+        rows = cb.rearrange("(g p t) c -> g t p c", g=PASSES, t=PACK)
+
+        def load_book(g, t):
+            nc.sync.dma_start(out=books[g][t][:], in_=rows[g, t])
+
+        nc.scalar.dma_start(out=norm_row[:], in_=norm[0:1, :].rearrange("o (b p j) -> p (o b) j", b=2, j=4))
+        nc.sync.dma_start(lists[0][:], offs)
+        for t in range(PACK):
+            load_book(0, t)
+        nc.sync.dma_start(lists[1][:], offs2)
+        load_book(1, 0)
+        load_book(1, 1)
+        nc.sync.dma_start(out=q_raw[:], in_=qT[0].rearrange("(g p t) q -> p g t q", g=PASSES, t=PACK))
+        load_book(1, 2)
+        load_book(1, 3)
+
+        make_identity(nc, ident[:])
+        for b in range(2):
+            for j in range(4):
+                nc.tensor.transpose(norm_bank[b][:, j, :], norm_row[:, b, j : j + 1].to_broadcast([P, P]), ident[:])
+            nc.scalar.copy(
+                norm_all[:, 512 * b : 512 * (b + 1)].rearrange("p (r j) -> p r j", j=4),
+                norm_bank[b][:].rearrange("p j r -> p r j"),
+            )
+
+        def gather(g, t, n0, width):
+            nc.vector.tensor_tensor(
+                raw[g][:, t, n0 : n0 + width],
+                books[g][t][:].indirect(lists[g][:, n0 // 16 : (n0 + width) // 16]),
+                norm_all[:, n0 : n0 + width],
+                MULT,
+            )
+
+        def interleave(copy, g, n0, width):
+            copy(
+                grouped[g][:, n0 : n0 + width, :].rearrange("p (c i) t -> p c t i", i=4),
+                raw[g][:, :, n0 : n0 + width].rearrange("p t (c i) -> p c t i", i=4),
+            )
+
+        def quantize(g, n0, width):
+            nc.vector.quantize_mx(
+                out=codes[g][:, n0 : n0 + width].bitcast(FP8X4),
+                scales=scales[g][:, n0 : n0 + width],
+                in_=grouped[g][:, n0 : n0 + width, :].rearrange("p n t -> p (n t)"),
+            )
+
+        def multiply(g, i):
+            n0, width = PIECES[i]
+            nc.tensor.matmul_mx(
+                out=acc[i][:],
+                lhsT=q_codes[:, g, :].bitcast(FP8X4),
+                lhsT_scale=q_scales[:, g, :],
+                rhs=codes[g][:, n0 : n0 + width].bitcast(FP8X4),
+                rhs_scale=scales[g][:, n0 : n0 + width],
+                start=(g == 0),
+                stop=(g == PASSES - 1),
+            )
+
+        def store(copy, i):
+            n0, width = PIECES[i]
+            copy(result[i][:], acc[i][:])
+            nc.sync.dma_start(out=out[0, :, n0 : n0 + width], in_=result[i][:])
+
+        for t in range(PACK):
+            gather(0, t, 0, 512)
+            gather(0, t, 512, 512)
+        interleave(nc.scalar.copy, 0, 0, 512)
+        interleave(nc.scalar.copy, 0, 512, 512)
+        gather(1, 0, 0, 512)
+        gather(1, 0, 512, 512)
+        quantize(0, 0, 512)
+        for g in range(PASSES):
+            nc.scalar.copy(
+                q_grouped[:, g].rearrange("p (c i) t -> p c t i", i=4),
+                q_raw[:, g].rearrange("p t (c i) -> p c t i", i=4),
+            )
+        gather(1, 1, 0, 512)
+        quantize(0, 512, 512)
+        nc.vector.quantize_mx(
+            out=q_codes[:].rearrange("p g q -> p (g q)").bitcast(FP8X4),
+            scales=q_scales[:].rearrange("p g q -> p (g q)"),
+            in_=q_grouped[:].rearrange("p g q t -> p (g q t)"),
+        )
+        gather(1, 2, 0, 512)
+        for i in range(4):
+            multiply(0, i)
+        gather(1, 3, 0, 512)
+        interleave(nc.scalar.copy, 1, 0, 512)
+        gather(1, 1, 512, 512)
+        for i in (1, 2, 3):
+            n0, width = PIECES[i]
+            gather(1, 2, n0, width)
+            gather(1, 3, n0, width)
+            interleave(nc.vector.tensor_copy if i == 3 else nc.scalar.copy, 1, n0, width)
+            p0, pwidth = PIECES[i - 1]
+            quantize(1, p0, pwidth)
+            multiply(1, i - 1)
+            store(nc.scalar.copy, i - 1)
+        quantize(1, 896, 128)
+        multiply(1, 3)
+        store(nc.vector.tensor_copy, 3)

@@ -20,7 +20,7 @@ CODES = 2048
 PASSES = D // (P * PACK)
 FLOPS = 2 * NQ * D * N
 
-PIECES = ((0, 512), (512, 256), (768, 128), (896, 128))
+PIECES = ((0, 512), (512, 256), (768, 256))
 
 
 def tile_attend_pq_att_kernel(tc, qT, cb, norm, offs, offs2, out):
@@ -51,16 +51,16 @@ def tile_attend_pq_att_kernel(tc, qT, cb, norm, offs, offs2, out):
         def load_book(g, t):
             nc.sync.dma_start(out=books[g][t][:], in_=rows[g, t])
 
-        nc.scalar.dma_start(out=norm_row[:], in_=norm[0:1, :].rearrange("o (b p j) -> p (o b) j", b=2, j=4))
+        nc.sync.dma_start(out=norm_row[:], in_=norm[0:1, :].rearrange("o (b p j) -> p (o b) j", b=2, j=4))
+        load_book(0, 0)
         nc.sync.dma_start(lists[0][:], offs)
-        for t in range(PACK):
+        for t in (1, 2, 3):
             load_book(0, t)
         nc.sync.dma_start(lists[1][:], offs2)
         load_book(1, 0)
-        load_book(1, 1)
         nc.sync.dma_start(out=q_raw[:], in_=qT[0].rearrange("(g p t) q -> p g t q", g=PASSES, t=PACK))
-        load_book(1, 2)
-        load_book(1, 3)
+        for t in (1, 2, 3):
+            load_book(1, t)
 
         make_identity(nc, ident[:])
         for b in range(2):
@@ -79,10 +79,10 @@ def tile_attend_pq_att_kernel(tc, qT, cb, norm, offs, offs2, out):
                 MULT,
             )
 
-        def interleave(copy, g, n0, width):
+        def interleave(copy, g, n0, width, t0=0, t1=PACK):
             copy(
-                grouped[g][:, n0 : n0 + width, :].rearrange("p (c i) t -> p c t i", i=4),
-                raw[g][:, :, n0 : n0 + width].rearrange("p t (c i) -> p c t i", i=4),
+                grouped[g][:, n0 : n0 + width, t0:t1].rearrange("p (c i) t -> p c t i", i=4),
+                raw[g][:, t0:t1, n0 : n0 + width].rearrange("p t (c i) -> p c t i", i=4),
             )
 
         def quantize(g, n0, width):
@@ -114,36 +114,34 @@ def tile_attend_pq_att_kernel(tc, qT, cb, norm, offs, offs2, out):
             gather(0, t, 512, 512)
         interleave(nc.scalar.copy, 0, 0, 512)
         interleave(nc.scalar.copy, 0, 512, 512)
-        gather(1, 0, 0, 512)
-        gather(1, 0, 512, 512)
+        gather(1, 0, 0, 768)
         quantize(0, 0, 512)
         for g in range(PASSES):
             nc.scalar.copy(
                 q_grouped[:, g].rearrange("p (c i) t -> p c t i", i=4),
                 q_raw[:, g].rearrange("p t (c i) -> p c t i", i=4),
             )
-        gather(1, 1, 0, 512)
+        gather(1, 1, 0, 768)
         quantize(0, 512, 512)
+        interleave(nc.scalar.copy, 1, 0, 768, 0, 2)
+        gather(1, 2, 0, 768)
         nc.vector.quantize_mx(
             out=q_codes[:].rearrange("p g q -> p (g q)").bitcast(FP8X4),
             scales=q_scales[:].rearrange("p g q -> p (g q)"),
             in_=q_grouped[:].rearrange("p g q t -> p (g q t)"),
         )
-        gather(1, 2, 0, 512)
-        for i in range(4):
+        for i in range(len(PIECES)):
             multiply(0, i)
-        gather(1, 3, 0, 512)
-        interleave(nc.scalar.copy, 1, 0, 512)
-        gather(1, 1, 512, 512)
-        for i in (1, 2, 3):
-            n0, width = PIECES[i]
-            gather(1, 2, n0, width)
+        for n0, width in ((0, 512), (512, 256)):
             gather(1, 3, n0, width)
-            interleave(nc.vector.tensor_copy if i == 3 else nc.scalar.copy, 1, n0, width)
-            p0, pwidth = PIECES[i - 1]
-            quantize(1, p0, pwidth)
-            multiply(1, i - 1)
-            store(nc.scalar.copy, i - 1)
-        quantize(1, 896, 128)
-        multiply(1, 3)
-        store(nc.vector.tensor_copy, 3)
+            interleave(nc.scalar.copy, 1, n0, width, 2, 4)
+        gather(1, 0, 768, 256)
+        gather(1, 1, 768, 256)
+        interleave(nc.scalar.copy, 1, 768, 256, 0, 2)
+        gather(1, 2, 768, 256)
+        gather(1, 3, 768, 256)
+        interleave(nc.scalar.copy, 1, 768, 256, 2, 4)
+        for i, (n0, width) in enumerate(PIECES):
+            quantize(1, n0, width)
+            multiply(1, i)
+            store(nc.vector.tensor_copy if i == 2 else nc.scalar.copy, i)

@@ -34,8 +34,10 @@ def tile_attend_pq_att_kernel(tc, qT, cb, norm, offs, offs2, out):
         norm_row = hold.tile([P, 2, 4], F32, name="norm_row")
         q_raw = hold.tile([P, PASSES, PACK, NQ], F32, name="q_raw")
         ident = hold.tile([P, P], F32, name="ident")
-        norm_all = hold.tile([P, N], F32, name="norm_all")
-        raw = [hold.tile([P, PACK, N], F32, name=f"raw{g}") for g in range(PASSES)]
+        norm_low = hold.tile([P, 768], F32, name="norm_low", tag="low")
+        norm_high = hold.tile([P, 256], F32, name="norm_high")
+        raw_low = [hold.tile([P, PACK, 768], F32, name=f"raw_low{g}") for g in range(PASSES)]
+        raw_high = [hold.tile([P, PACK, 256], F32, name="raw_high0")]
         grouped = [hold.tile([P, N, PACK], BF16, name=f"grouped{g}", align_bytes=64) for g in range(PASSES)]
         codes = [hold.tile([P, N], U32, name=f"codes{g}", align_bytes=64) for g in range(PASSES)]
         scales = [hold.tile([P, N], U8, name=f"scales{g}", align_bytes=64) for g in range(PASSES)]
@@ -57,32 +59,47 @@ def tile_attend_pq_att_kernel(tc, qT, cb, norm, offs, offs2, out):
         for t in (1, 2, 3):
             load_book(0, t)
         nc.sync.dma_start(lists[1][:], offs2)
-        load_book(1, 0)
-        nc.sync.dma_start(out=q_raw[:], in_=qT[0].rearrange("(g p t) q -> p g t q", g=PASSES, t=PACK))
-        for t in (1, 2, 3):
+        for t in (0, 1, 2):
             load_book(1, t)
+        nc.sync.dma_start(out=q_raw[:], in_=qT[0].rearrange("(g p t) q -> p g t q", g=PASSES, t=PACK))
+        load_book(1, 3)
 
         make_identity(nc, ident[:])
         for b in range(2):
             for j in range(4):
                 nc.tensor.transpose(norm_bank[b][:, j, :], norm_row[:, b, j : j + 1].to_broadcast([P, P]), ident[:])
-            nc.scalar.copy(
-                norm_all[:, 512 * b : 512 * (b + 1)].rearrange("p (r j) -> p r j", j=4),
-                norm_bank[b][:].rearrange("p j r -> p r j"),
-            )
+        nc.scalar.copy(
+            norm_low[:, 0:512].rearrange("p (r j) -> p r j", j=4),
+            norm_bank[0][:].rearrange("p j r -> p r j"),
+        )
+        nc.scalar.copy(
+            norm_low[:, 512:768].rearrange("p (r j) -> p r j", j=4),
+            norm_bank[1][:, :, 0:64].rearrange("p j r -> p r j"),
+        )
+        nc.scalar.copy(
+            norm_high[:].rearrange("p (r j) -> p r j", j=4),
+            norm_bank[1][:, :, 64:128].rearrange("p j r -> p r j"),
+        )
+
+        def columns(g, n0, width):
+            if n0 < 768:
+                return raw_low[g], slice(n0, n0 + width)
+            return raw_high[g], slice(n0 - 768, n0 - 768 + width)
 
         def gather(g, t, n0, width):
+            tile, cols = columns(g, n0, width)
             nc.vector.tensor_tensor(
-                raw[g][:, t, n0 : n0 + width],
+                tile[:, t, cols],
                 books[g][t][:].indirect(lists[g][:, n0 // 16 : (n0 + width) // 16]),
-                norm_all[:, n0 : n0 + width],
+                norm_low[:, cols] if n0 < 768 else norm_high[:, cols],
                 MULT,
             )
 
-        def interleave(copy, g, n0, width, t0=0, t1=PACK):
+        def interleave(copy, g, n0, width):
+            tile, cols = columns(g, n0, width)
             copy(
-                grouped[g][:, n0 : n0 + width, t0:t1].rearrange("p (c i) t -> p c t i", i=4),
-                raw[g][:, t0:t1, n0 : n0 + width].rearrange("p t (c i) -> p c t i", i=4),
+                grouped[g][:, n0 : n0 + width, :].rearrange("p (c i) t -> p c t i", i=4),
+                tile[:, :, cols].rearrange("p t (c i) -> p c t i", i=4),
             )
 
         def quantize(g, n0, width):
@@ -109,22 +126,23 @@ def tile_attend_pq_att_kernel(tc, qT, cb, norm, offs, offs2, out):
             copy(result[i][:], acc[i][:])
             nc.sync.dma_start(out=out[0, :, n0 : n0 + width], in_=result[i][:])
 
-        for t in range(PACK):
-            gather(0, t, 0, 512)
-            gather(0, t, 512, 512)
-        interleave(nc.scalar.copy, 0, 0, 512)
-        interleave(nc.scalar.copy, 0, 512, 512)
+        gather(0, 0, 0, 512)
+        gather(0, 0, 512, 256)
+        gather(0, 0, 768, 256)
+        for t in (1, 2, 3):
+            gather(0, t, 0, 768)
+            gather(0, t, 768, 256)
+        interleave(nc.scalar.copy, 0, 0, 768)
+        interleave(nc.scalar.copy, 0, 768, 256)
         gather(1, 0, 0, 768)
-        quantize(0, 0, 512)
         for g in range(PASSES):
             nc.scalar.copy(
                 q_grouped[:, g].rearrange("p (c i) t -> p c t i", i=4),
                 q_raw[:, g].rearrange("p t (c i) -> p c t i", i=4),
             )
         gather(1, 1, 0, 768)
-        quantize(0, 512, 512)
-        interleave(nc.scalar.copy, 1, 0, 768, 0, 2)
         gather(1, 2, 0, 768)
+        quantize(0, 0, N)
         nc.vector.quantize_mx(
             out=q_codes[:].rearrange("p g q -> p (g q)").bitcast(FP8X4),
             scales=q_scales[:].rearrange("p g q -> p (g q)"),
@@ -134,13 +152,11 @@ def tile_attend_pq_att_kernel(tc, qT, cb, norm, offs, offs2, out):
             multiply(0, i)
         for n0, width in ((0, 512), (512, 256)):
             gather(1, 3, n0, width)
-            interleave(nc.scalar.copy, 1, n0, width, 2, 4)
-        gather(1, 0, 768, 256)
-        gather(1, 1, 768, 256)
-        interleave(nc.scalar.copy, 1, 768, 256, 0, 2)
-        gather(1, 2, 768, 256)
-        gather(1, 3, 768, 256)
-        interleave(nc.scalar.copy, 1, 768, 256, 2, 4)
+            interleave(nc.scalar.copy, 1, n0, width)
+        raw_high.append(hold.tile([P, PACK, 256], F32, name="raw_high1", tag="low"))
+        for t in range(PACK):
+            gather(1, t, 768, 256)
+        interleave(nc.scalar.copy, 1, 768, 256)
         for i, (n0, width) in enumerate(PIECES):
             quantize(1, n0, width)
             multiply(1, i)

from contextlib import ExitStack

import concourse.mybir as mybir
from concourse.masks import make_identity

F32 = mybir.dt.float32
BF16 = mybir.dt.bfloat16
U32 = mybir.dt.uint32
U16 = mybir.dt.uint16
U8 = mybir.dt.uint8
FP8X4 = mybir.dt.float8_e4m3fn_x4
MULT = mybir.AluOpType.mult

P = 128
PACK = 4
D = 1024
N = 1024
NQ = 128
CODES = 2048
PASSES = D // (P * PACK)
FLOPS = 2 * NQ * D * N

PIECES = ((0, 512), (512, 256), (768, 256))


def tile_attend_pq_att_kernel(tc, qT, cb, norm, offs, offs2, out):
    nc = tc.nc
    with ExitStack() as ctx:
        hold = ctx.enter_context(tc.tile_pool(name="hold", bufs=1))
        psum = ctx.enter_context(tc.psum_pool(name="psum", bufs=1))

        lists = [hold.tile([P, N // 16], U16, name=f"list{g}") for g in range(PASSES)]
        books = [[hold.tile([P, CODES], F32, name=f"book{g}_{t}") for t in range(PACK)] for g in range(PASSES)]
        norm_row = hold.tile([P, 2, 4], F32, name="norm_row")
        q_raw = hold.tile([P, PASSES, PACK, NQ], F32, name="q_raw")
        ident = hold.tile([P, P], F32, name="ident")
        norm_low = hold.tile([P, 768], F32, name="norm_low", tag="low")
        norm_high = hold.tile([P, 256], F32, name="norm_high")
        raw_low = [hold.tile([P, PACK, 768], F32, name=f"raw_low{g}") for g in range(PASSES)]
        raw_high = [hold.tile([P, PACK, 256], F32, name="raw_high0")]
        grouped = [hold.tile([P, N, PACK], BF16, name=f"grouped{g}", align_bytes=64) for g in range(PASSES)]
        codes = [hold.tile([P, N], U32, name=f"codes{g}", align_bytes=64) for g in range(PASSES)]
        scales = [hold.tile([P, N], U8, name=f"scales{g}", align_bytes=64) for g in range(PASSES)]
        q_grouped = hold.tile([P, PASSES, NQ, PACK], BF16, name="q_grouped", align_bytes=64)
        q_codes = hold.tile([P, PASSES, NQ], U32, name="q_codes", align_bytes=64)
        q_scales = hold.tile([P, PASSES, NQ], U8, name="q_scales", align_bytes=64)
        result = [hold.tile([P, width], F32, name=f"result{i}") for i, (n0, width) in enumerate(PIECES)]
        norm_bank = [psum.tile([P, 4, P], F32, name=f"norm_bank{b}") for b in range(2)]
        acc = [psum.tile([P, width], F32, name=f"acc{i}") for i, (n0, width) in enumerate(PIECES)]

        rows = cb.rearrange("(g p t) c -> g t p c", g=PASSES, t=PACK)

        def load_book(g, t):
            nc.sync.dma_start(out=books[g][t][:], in_=rows[g, t])

        nc.sync.dma_start(out=norm_row[:], in_=norm[0:1, :].rearrange("o (b p j) -> p (o b) j", b=2, j=4))
        load_book(0, 0)
        nc.sync.dma_start(lists[0][:], offs)
        for t in (1, 2, 3):
            load_book(0, t)
        nc.sync.dma_start(lists[1][:], offs2)
        for t in (0, 1, 2):
            load_book(1, t)
        nc.sync.dma_start(out=q_raw[:], in_=qT[0].rearrange("(g p t) q -> p g t q", g=PASSES, t=PACK))
        load_book(1, 3)

        make_identity(nc, ident[:])
        for b in range(2):
            for j in range(4):
                nc.tensor.transpose(norm_bank[b][:, j, :], norm_row[:, b, j : j + 1].to_broadcast([P, P]), ident[:])
        nc.scalar.copy(
            norm_low[:, 0:512].rearrange("p (r j) -> p r j", j=4),
            norm_bank[0][:].rearrange("p j r -> p r j"),
        )
        nc.scalar.copy(
            norm_low[:, 512:768].rearrange("p (r j) -> p r j", j=4),
            norm_bank[1][:, :, 0:64].rearrange("p j r -> p r j"),
        )
        nc.scalar.copy(
            norm_high[:].rearrange("p (r j) -> p r j", j=4),
            norm_bank[1][:, :, 64:128].rearrange("p j r -> p r j"),
        )

        def columns(g, n0, width):
            if n0 < 768:
                return raw_low[g], slice(n0, n0 + width)
            return raw_high[g], slice(n0 - 768, n0 - 768 + width)

        def gather(g, t, n0, width):
            tile, cols = columns(g, n0, width)
            nc.vector.tensor_tensor(
                tile[:, t, cols],
                books[g][t][:].indirect(lists[g][:, n0 // 16 : (n0 + width) // 16]),
                norm_low[:, cols] if n0 < 768 else norm_high[:, cols],
                MULT,
            )

        def interleave(copy, g, n0, width):
            tile, cols = columns(g, n0, width)
            copy(
                grouped[g][:, n0 : n0 + width, :].rearrange("p (c i) t -> p c t i", i=4),
                tile[:, :, cols].rearrange("p t (c i) -> p c t i", i=4),
            )

        def quantize(g, n0, width):
            nc.vector.quantize_mx(
                out=codes[g][:, n0 : n0 + width].bitcast(FP8X4),
                scales=scales[g][:, n0 : n0 + width],
                in_=grouped[g][:, n0 : n0 + width, :].rearrange("p n t -> p (n t)"),
            )

        def multiply(g, i):
            n0, width = PIECES[i]
            nc.tensor.matmul_mx(
                out=acc[i][:],
                lhsT=q_codes[:, g, :].bitcast(FP8X4),
                lhsT_scale=q_scales[:, g, :],
                rhs=codes[g][:, n0 : n0 + width].bitcast(FP8X4),
                rhs_scale=scales[g][:, n0 : n0 + width],
                start=(g == 0),
                stop=(g == PASSES - 1),
            )

        def store(copy, i):
            n0, width = PIECES[i]
            copy(result[i][:], acc[i][:])
            nc.sync.dma_start(out=out[0, :, n0 : n0 + width], in_=result[i][:])

        gather(0, 0, 0, 512)
        gather(0, 0, 512, 256)
        gather(0, 0, 768, 256)
        for t in (1, 2, 3):
            gather(0, t, 0, 768)
            gather(0, t, 768, 256)
        interleave(nc.scalar.copy, 0, 0, 768)
        interleave(nc.scalar.copy, 0, 768, 256)
        gather(1, 0, 0, 768)
        for g in range(PASSES):
            nc.scalar.copy(
                q_grouped[:, g].rearrange("p (c i) t -> p c t i", i=4),
                q_raw[:, g].rearrange("p t (c i) -> p c t i", i=4),
            )
        gather(1, 1, 0, 768)
        gather(1, 2, 0, 768)
        quantize(0, 0, N)
        nc.vector.quantize_mx(
            out=q_codes[:].rearrange("p g q -> p (g q)").bitcast(FP8X4),
            scales=q_scales[:].rearrange("p g q -> p (g q)"),
            in_=q_grouped[:].rearrange("p g q t -> p (g q t)"),
        )
        for i in range(len(PIECES)):
            multiply(0, i)
        for n0, width in ((0, 512), (512, 256)):
            gather(1, 3, n0, width)
            interleave(nc.scalar.copy, 1, n0, width)
        raw_high.append(hold.tile([P, PACK, 256], F32, name="raw_high1", tag="low"))
        for t in range(PACK):
            gather(1, t, 768, 256)
        interleave(nc.scalar.copy, 1, 768, 256)
        for i, (n0, width) in enumerate(PIECES):
            quantize(1, n0, width)
            multiply(1, i)
            store(nc.vector.tensor_copy if i == 2 else nc.scalar.copy, i)
